import numpy as np
import ml_dtypes


def mxq(x, axis, fmt="e4m3"):
    dtype, down = {"e4m3": (ml_dtypes.float8_e4m3fn, 7), "e5m2": (ml_dtypes.float8_e5m2, 14)}[fmt]
    v = np.moveaxis(np.asarray(x, np.float32).astype(ml_dtypes.bfloat16).astype(np.float64), axis, -1)
    blocks = v.reshape(v.shape[:-1] + (-1, 32))
    amax = np.abs(blocks).max(-1, keepdims=True)
    byte = np.maximum(np.where(amax > 0, np.frexp(amax)[1] - 1 + 127, 0) - down, 1)
    scale = np.exp2(byte - 127.0)
    codes = (blocks / scale).astype(np.float32).astype(dtype).astype(np.float64)
    return np.moveaxis((codes * scale).reshape(v.shape), -1, axis)


WIDE = False


def mx_kscale(k):
    if not WIDE:
        return np.ones(k)
    levels = np.array([10, -10, 5, -5, 0])
    if k % 512:
        return np.exp2(np.random.permutation(np.resize(levels, k // 32))).repeat(32)
    a = np.empty((k // 512, 16))
    for p in range(k // 512):
        a[p, :8] = np.random.permutation(np.resize(levels, 8))
        for g in range(8):
            far = levels[np.abs(levels - a[p, g]) >= 10]
            a[p, g + 8] = far[np.random.randint(len(far))]
    return np.exp2(a.ravel()).repeat(32)


def f64(x):
    return np.asarray(x).astype(np.float64)


def striped(idx):
    return np.tile(idx.reshape(-1, 16).T, (8, 1)).astype(np.uint16)


def unstriped(offs):
    return offs[:16].T.reshape(-1).astype(np.int64)


def striped8(idx):
    return np.concatenate([x.reshape(-1, 16).T for x in idx]).astype(np.uint16)


def runs(offs, k):
    lists = np.stack([offs[16 * r : 16 * r + 16].T.reshape(-1) for r in range(8)]).astype(np.int64)
    return lists[np.arange(k) % 512 // 64]


def pack_weight(w):
    k, n = w.shape
    w = f64(np.asarray(w, np.float32).astype(ml_dtypes.bfloat16)).reshape(k // 32, 32, n)
    amax = np.abs(w).max(1)
    byte = np.clip(np.where(amax > 0, np.frexp(amax)[1] - 1 + 127 - 7, 1), 1, 254)
    scaled = (w * np.exp2(127.0 - byte)[:, None, :]).reshape(k, n).astype(np.float32)
    words = np.ascontiguousarray(scaled.reshape(k // 512, 128, 4, n).transpose(0, 1, 3, 2)).astype(ml_dtypes.float8_e4m3fn).view(np.uint8)
    return words, np.ascontiguousarray(byte.astype(np.uint8).reshape(k // 512, 16, n))


def unpack_weight(words, scales):
    g, p, n, _ = words.shape
    vals = np.ascontiguousarray(words).view(ml_dtypes.float8_e4m3fn).astype(np.float64) * np.repeat(np.exp2(scales.astype(np.float64) - 127.0), 8, axis=1)[..., None]
    return vals.transpose(0, 1, 3, 2).reshape(g * 512, n)


E2M1 = np.array([0.0, 0.5, 1.0, 1.5, 2.0, 3.0, 4.0, 6.0, -0.0, -0.5, -1.0, -1.5, -2.0, -3.0, -4.0, -6.0])


def pack_fp4(w):
    k, n = w.shape
    w = f64(np.asarray(w, np.float32).astype(ml_dtypes.bfloat16)).reshape(k // 32, 32, n)
    amax = np.abs(w).max(1)
    mant, ex = np.frexp(amax / 6.0)
    byte = np.clip(np.where(amax > 0, np.where(mant > 0.5, ex, ex - 1) + 127, 1), 1, 254)
    scaled = (w * np.exp2(127.0 - byte)[:, None, :]).reshape(k, n).astype(np.float32)
    c = np.ascontiguousarray(scaled.reshape(k // 512, 128, 4, n).transpose(0, 1, 3, 2)).astype(ml_dtypes.float4_e2m1fn).view(np.uint8) & 0xF
    words = (c[..., 0::2] | (c[..., 1::2] << 4)).reshape(k // 512, 128, 2 * n)
    return np.ascontiguousarray(words), np.ascontiguousarray(byte.astype(np.uint8).reshape(k // 512, 16, n))


def unpack_fp4(words, scales):
    g, _, n = scales.shape
    words = np.ascontiguousarray(words).reshape(g, 128, n, 2)
    nib = np.empty((g, 128, n, 4), np.uint8)
    nib[..., 0::2] = words & 0xF
    nib[..., 1::2] = words >> 4
    vals = E2M1[nib] * np.repeat(np.exp2(scales.astype(np.float64) - 127.0), 8, axis=1)[..., None]
    return vals.transpose(0, 1, 3, 2).reshape(g * 512, n)


def sigmoid(v):
    return 1.0 / (1.0 + np.exp(-np.maximum(v, -700.0)))

def planes(y):
    n, m = y.shape
    v = y.astype(np.float32).astype(ml_dtypes.bfloat16).astype(np.float64).reshape(n // 32, 32, m)
    top = np.abs(v).max(1)
    byte = np.clip(np.where(top > 0, np.frexp(top)[1] - 1 + 127 - 7, 1), 1, 254)
    codes = (v * np.exp2(127.0 - byte)[:, None, :]).reshape(n, m).astype(np.float32).astype(ml_dtypes.float8_e4m3fn).view(np.uint8)
    words = codes.reshape(n // 512, 128, 4, m).transpose(0, 1, 3, 2)
    return np.ascontiguousarray(words), np.ascontiguousarray(byte.astype(np.uint8).reshape(n // 512, 16, m))


K, T, S, N, H, J = 512, 2048, 512, 512, 512, 512


def setup_inputs():
    n = np.random.standard_normal
    s = mx_kscale(K)[:, None]
    u = mx_kscale(H)
    packed_xT = pack_weight(n((K, T)) * s)
    packed_w1 = pack_fp4(n((K, H)) / np.sqrt(K) / s)
    packed_w2 = pack_fp4(n((K, H)) / np.sqrt(K) / s)
    packed_w3 = pack_fp4(n((H, N)) / np.sqrt(H) / u[:, None])
    return {
        "x_words": packed_xT[0],
        "x_scales": packed_xT[1],
        "w1_words": packed_w1[0],
        "w1_scales": packed_w1[1],
        "w2_words": packed_w2[0],
        "w2_scales": packed_w2[1],
        "gn": (np.random.uniform(0.5, 1.5, (H, 1)) * u[:, None]).astype(np.float32),
        "w3_words": packed_w3[0],
        "w3_scales": packed_w3[1],
        "tab": n((N, J)).astype(np.float32),
        "offs": striped(np.random.permutation(T)[:S]),
        "two": striped(np.random.permutation(T)[:S]),
        "n1": striped8(np.stack([np.random.permutation(S) for _ in range(8)])),
        "n2": striped8(np.stack([np.random.permutation(S) for _ in range(8)])),
        "n3": striped8(np.random.randint(0, J, (8, S))),
        "n4": striped8(np.stack([np.random.permutation(S) for _ in range(8)])),
    }


def reference(x_words, x_scales, w1_words, w1_scales, w2_words, w2_scales, gn, w3_words, w3_scales, tab, offs, two, n1, n2, n3, n4):
    xq = unpack_weight(x_words, x_scales)[:, unstriped(offs)]
    y = unpack_fp4(w1_words, w1_scales).T @ xq
    x_two = unpack_weight(x_words, x_scales)[:, unstriped(two)]
    d = unpack_fp4(w2_words, w2_scales).T @ x_two
    z = f64(gn) * (y + (sigmoid(d[np.arange(H)[:, None], runs(n2, H)] - d)) * (y[np.arange(H)[:, None], runs(n1, H)] - y))
    h = unpack_fp4(w3_words, w3_scales).T @ mxq(z, 0, "e4m3")
    out_0 = np.maximum(h + f64(tab)[np.arange(N)[:, None], runs(n3, N)], h[np.arange(N)[:, None], runs(n4, N)])
    return (out_0,) + planes(out_0)

@@ -1,0 +1,190 @@
+from contextlib import ExitStack
+
+import concourse.mybir as mybir
+
+K, T, S, N, H, J = 512, 2048, 512, 512, 512, 512
+FLOPS = 2 * S * (K * H + K * H + H * N)
+
+F32 = mybir.dt.float32
+BF16 = mybir.dt.bfloat16
+I32 = mybir.dt.int32
+U32 = mybir.dt.uint32
+U16 = mybir.dt.uint16
+U8 = mybir.dt.uint8
+FP8X4 = mybir.dt.float8_e4m3fn_x4
+FP4X4 = mybir.dt.float4_e2m1fn_x4
+ALU = mybir.AluOpType
+ACT = mybir.ActivationFunctionType
+
+P = 128
+PACK = 4
+HALF = S // 2
+PIECES = ((0, 256), (256, 384), (384, 512))
+
+
+def tile_picked_twlpullbkind_none_po_kernel(
+    tc, x_words, x_scales, w1_words, w1_scales, w2_words, w2_scales, gn, w3_words, w3_scales,
+    tab, offs, two, n1, n2, n3, n4, out_0, out_1, out_2,
+):
+    nc = tc.nc
+    with ExitStack() as ctx:
+        keep = ctx.enter_context(tc.tile_pool(name="keep", bufs=1))
+        psum = ctx.enter_context(tc.psum_pool(name="psum", bufs=8))
+
+        def tile(shape, dtype, name):
+            return keep.tile(shape, dtype, name=name, align_bytes=64)
+
+        def load_list(src, name):
+            dst = tile([P, S // 16], U16, name)
+            nc.sync.dma_start(dst[:], src)
+            return dst
+
+        def load_scale_rows(queue, dst, src):
+            for q in range(4):
+                queue.dma_start(out=dst[32 * q : 32 * q + 4, :].bitcast(I32), in_=src[0, 4 * q : 4 * q + 4, :].bitcast(I32))
+
+        def entries(lst, lo, hi):
+            return lst[:, lo // 16 : hi // 16]
+
+        warm = tile([P, 2], F32, "warm")
+        nc.gpsimd.memset(warm[:, 0:1], 0.0)
+        nc.scalar.activation(warm[:, 1:2], warm[:, 0:1], ACT.Sigmoid)
+
+        xs = tile([P, T], U8, "xs")
+        nc.vector.memset(xs[:].bitcast(I32), 0)
+        ws_raw = tile([P, H], U8, "ws_raw")
+        nc.gpsimd.memset(ws_raw[:].bitcast(I32), 0)
+        ww_raw = tile([P, 2 * H], U8, "ww_raw")
+        xw = keep.tile([P, T], I32, name="xw", tag="table0", align_bytes=64)
+
+        def load_weight(words, scales):
+            nc.sync.dma_start(out=ww_raw[:].bitcast(I32), in_=words[0].bitcast(I32))
+            load_scale_rows(nc.sync, ws_raw, scales)
+
+        def deal(name):
+            words = tile([P, PACK, P, 2], U8, name + "_words")
+            nc.vector.tensor_copy(out=words[:], in_=ww_raw[:].rearrange("p (m t b) -> p t m b", t=PACK, b=2))
+            scales = tile([P, PACK, P], U8, name + "_scales")
+            nc.vector.tensor_copy(out=scales[:], in_=ws_raw[:].rearrange("p (m t) -> p t m", t=PACK))
+            return words, scales
+
+        nc.sync.dma_start(out=xw[:], in_=x_words[0].rearrange("p n t -> p (n t)").bitcast(I32))
+        load_scale_rows(nc.scalar, xs, x_scales)
+        two_l = load_list(two, "two_l")
+        load_weight(w2_words, w2_scales)
+        offs_l = load_list(offs, "offs_l")
+        n2_l = load_list(n2, "n2_l")
+        gain = tile([P, PACK], F32, "gain")
+        nc.gpsimd.dma_start(out=gain[:], in_=gn.rearrange("(p t) o -> p (t o)", t=PACK))
+        n1_l = load_list(n1, "n1_l")
+        n3_l = load_list(n3, "n3_l")
+        n4_l = load_list(n4, "n4_l")
+
+        def pick(lst, name, slots):
+            scales = keep.tile([P, S], U8, name=name + "_scales", tag=slots[0], align_bytes=64)
+            nc.vector.tensor_copy(out=scales[:], in_=xs[:].indirect(lst[:]))
+            words = keep.tile([P, S], U32, name=name + "_words", tag=slots[1], align_bytes=64)
+            nc.vector.tensor_copy(out=words[:], in_=xw[:].bitcast(U32).indirect(lst[:]))
+            return words, scales
+
+        def product(w, t, words, scales):
+            bank = psum.tile([P, words.shape[1]], F32, name="bank")
+            nc.tensor.matmul_mx(
+                out=bank[:],
+                lhsT=w[0][:, t, :, :].rearrange("p m b -> p (m b)").bitcast(FP4X4),
+                lhsT_scale=w[1][:, t, :],
+                rhs=words[:].bitcast(FP8X4),
+                rhs_scale=scales[:],
+                start=True,
+                stop=True,
+            )
+            return bank
+
+        w2 = deal("w2")
+        load_weight(w1_words, w1_scales)
+        x_two = pick(two_l, "x_two", ("table1", "table2"))
+        x_idx = pick(offs_l, "x_idx", ("table3", "idx_words"))
+        d_win, d_plain = [], []
+        for t in range(PACK):
+            bank = product(w2, t, *x_two)
+            win = tile([P, S], F32, "d_win%d" % t)
+            nc.scalar.copy(out=win[:], in_=bank[:])
+            plain = tile([P, S], F32, "d_plain%d" % t)
+            nc.scalar.copy(out=plain[:], in_=bank[:])
+            d_win.append(win)
+            d_plain.append(plain)
+        w1 = deal("w1")
+        load_weight(w3_words, w3_scales)
+        tab_rows = tab.rearrange("(p t) c -> p t c", t=PACK)
+        tab_win = []
+        for t in range(PACK):
+            win = keep.tile([P, J], F32, name="tab_win%d" % t, tag="table%d" % t, align_bytes=64)
+            nc.sync.dma_start(out=win[:], in_=tab_rows[:, t, :])
+            tab_win.append(win)
+        gate, y_win = [], []
+        for t in range(PACK):
+            diff = tile([P, S], F32, "diff%d" % t)
+            for lo in (0, HALF):
+                cols = slice(lo, lo + HALF)
+                nc.vector.tensor_tensor(diff[:, cols], d_win[t][:].indirect(entries(n2_l, lo, lo + HALF)), d_plain[t][:, cols], ALU.subtract)
+            gate.append(diff)
+        for t in range(PACK):
+            bank = product(w1, t, *x_idx)
+            g = tile([P, S], F32, "gate%d" % t)
+            nc.scalar.activation(g[:], gate[t][:], ACT.Sigmoid)
+            gate[t] = g
+            win = tile([P, S], F32, "y_win%d" % t)
+            nc.scalar.activation(win[:], bank[:], ACT.Copy, scale=gain[:, t : t + 1])
+            y_win.append(win)
+        w3 = deal("w3")
+
+        h_win = [tile([P, S], F32, "h_win%d" % t) for t in range(PACK)]
+        for lo in (0, HALF):
+            cols = slice(lo, lo + HALF)
+            pulled = tile([P, PACK, HALF], F32, "pulled%d" % lo)
+            kept = tile([P, PACK, HALF], F32, "kept%d" % lo)
+            for t in range(PACK):
+                nc.vector.tensor_tensor(pulled[:, t, :], y_win[t][:].indirect(entries(n1_l, lo, lo + HALF)), gate[t][:, cols], ALU.mult)
+                nc.vector.scalar_tensor_tensor(kept[:, t, :], gate[t][:, cols], 1.0, y_win[t][:, cols], ALU.subtract, ALU.mult)
+            z = tile([P, HALF, PACK], BF16, "z%d" % lo)
+            nc.vector.tensor_tensor(
+                z[:].rearrange("p (c i) t -> p c t i", i=4),
+                pulled[:].rearrange("p t (c i) -> p c t i", i=4),
+                kept[:].rearrange("p t (c i) -> p c t i", i=4),
+                ALU.subtract,
+            )
+            z_words = tile([P, HALF], U32, "z_words%d" % lo)
+            z_scales = tile([P, HALF], U8, "z_scales%d" % lo)
+            nc.vector.quantize_mx(out=z_words[:].bitcast(FP8X4), scales=z_scales[:], in_=z[:].rearrange("p c t -> p (c t)"))
+            for t in range(PACK):
+                bank = product(w3, t, z_words, z_scales)
+                nc.scalar.copy(out=h_win[t][:, cols], in_=bank[:])
+
+        out_rows = out_0.rearrange("(p t) c -> p t c", t=PACK)
+        out_words = tile([P, S], U32, "out_words")
+        out_scales = tile([P, S], U8, "out_scales")
+        words_dram = out_1[0].rearrange("p n t -> p (n t)").bitcast(I32)
+        for lo, hi in PIECES:
+            cols = slice(lo, hi)
+            width = hi - lo
+            summed = tile([P, PACK, width], F32, "summed%d" % lo)
+            other = tile([P, PACK, width], F32, "other%d" % lo)
+            for t in range(PACK):
+                nc.vector.tensor_tensor(summed[:, t, :], tab_win[t][:].indirect(entries(n3_l, lo, hi)), h_win[t][:, cols], ALU.add)
+            for t in range(PACK):
+                nc.vector.tensor_copy(out=other[:, t, :], in_=h_win[t][:].indirect(entries(n4_l, lo, hi)))
+            result = tile([P, PACK, width], F32, "result%d" % lo)
+            nc.vector.tensor_tensor(result[:], summed[:], other[:], ALU.max)
+            nc.sync.dma_start(out=out_rows[:, :, cols], in_=result[:])
+            rounded = tile([P, width, PACK], BF16, "rounded%d" % lo)
+            dst = rounded[:].rearrange("p (c i) t -> p c t i", i=4)
+            src = result[:].rearrange("p t (c i) -> p c t i", i=4)
+            if hi < S:
+                nc.scalar.copy(out=dst, in_=src)
+            else:
+                nc.vector.tensor_copy(out=dst, in_=src)
+            nc.vector.quantize_mx(out=out_words[:, cols].bitcast(FP8X4), scales=out_scales[:, cols], in_=rounded[:].rearrange("p c t -> p (c t)"))
+            nc.sync.dma_start(out=words_dram[:, cols], in_=out_words[:, cols].bitcast(I32))
+        for q in range(4):
+            queue = nc.scalar if q % 2 == 0 else nc.sync
+            queue.dma_start(out=out_2[0, 4 * q : 4 * q + 4, :].bitcast(I32), in_=out_scales[32 * q : 32 * q + 4, :].bitcast(I32))

@@ -1,6 +1,7 @@
 from contextlib import ExitStack
 
 import concourse.mybir as mybir
+from concourse.masks import make_identity
 
 K, T, S, N, H, J = 512, 2048, 512, 512, 512, 512
 FLOPS = 2 * S * (K * H + K * H + H * N)
@@ -18,7 +19,6 @@ ACT = mybir.ActivationFunctionType
 
 P = 128
 PACK = 4
-HALF = S // 2
 PIECES = ((0, 256), (256, 384), (384, 512))
 
 
@@ -29,10 +29,10 @@ def tile_picked_twlpullbkind_none_po_kernel(
     nc = tc.nc
     with ExitStack() as ctx:
         keep = ctx.enter_context(tc.tile_pool(name="keep", bufs=1))
-        psum = ctx.enter_context(tc.psum_pool(name="psum", bufs=8))
+        psum = ctx.enter_context(tc.psum_pool(name="psum", bufs=1))
 
-        def tile(shape, dtype, name):
-            return keep.tile(shape, dtype, name=name, align_bytes=64)
+        def tile(shape, dtype, name, slot=None):
+            return keep.tile(shape, dtype, name=name, tag=slot or name, align_bytes=64)
 
         def load_list(src, name):
             dst = tile([P, S // 16], U16, name)
@@ -46,49 +46,70 @@ def tile_picked_twlpullbkind_none_po_kernel(
         def entries(lst, lo, hi):
             return lst[:, lo // 16 : hi // 16]
 
-        warm = tile([P, 2], F32, "warm")
-        nc.gpsimd.memset(warm[:, 0:1], 0.0)
-        nc.scalar.activation(warm[:, 1:2], warm[:, 0:1], ACT.Sigmoid)
+        def load_scales(src, name, engine, queue):
+            raw = tile([P, H], U8, name)
+            engine.memset(raw[:].bitcast(I32), 0)
+            load_scale_rows(queue, raw, src)
+            return raw
 
         xs = tile([P, T], U8, "xs")
         nc.vector.memset(xs[:].bitcast(I32), 0)
-        ws_raw = tile([P, H], U8, "ws_raw")
-        nc.gpsimd.memset(ws_raw[:].bitcast(I32), 0)
-        ww_raw = tile([P, 2 * H], U8, "ww_raw")
+        warm = tile([P, 2], F32, "warm")
+        nc.vector.memset(warm[:, 0:1], 0.0)
+        nc.scalar.activation(warm[:, 1:2], warm[:, 0:1], ACT.Sigmoid)
+
+        ident = tile([P, P], F32, "ident")
+        make_identity(nc, ident[:])
+
         xw = keep.tile([P, T], I32, name="xw", tag="table0", align_bytes=64)
 
-        def load_weight(words, scales):
-            nc.sync.dma_start(out=ww_raw[:].bitcast(I32), in_=words[0].bitcast(I32))
-            load_scale_rows(nc.sync, ws_raw, scales)
+        def load_words(src, name, slot):
+            raw = keep.tile([P, 2 * H], U8, name=name, tag=slot, align_bytes=64)
+            nc.sync.dma_start(out=raw[:].bitcast(I32), in_=src[0].bitcast(I32))
+            return raw
 
-        def deal(name):
-            words = tile([P, PACK, P, 2], U8, name + "_words")
-            nc.vector.tensor_copy(out=words[:], in_=ww_raw[:].rearrange("p (m t b) -> p t m b", t=PACK, b=2))
-            scales = tile([P, PACK, P], U8, name + "_scales")
-            nc.vector.tensor_copy(out=scales[:], in_=ws_raw[:].rearrange("p (m t) -> p t m", t=PACK))
-            return words, scales
+        def deal_words(engine, raw, name, slot=None):
+            words = tile([P, PACK, P, 2], U8, name, slot)
+            engine.tensor_copy(out=words[:], in_=raw[:].rearrange("p (m t b) -> p t m b", t=PACK, b=2))
+            return words
 
-        nc.sync.dma_start(out=xw[:], in_=x_words[0].rearrange("p n t -> p (n t)").bitcast(I32))
-        load_scale_rows(nc.scalar, xs, x_scales)
+        def deal_scales(engine, raw, name, slot=None):
+            scales = tile([P, PACK, P], U8, name, slot)
+            engine.tensor_copy(out=scales[:], in_=raw[:].rearrange("p (m t) -> p t m", t=PACK))
+            return scales
+
+        nc.scalar.dma_start(out=xw[:], in_=x_words[0].rearrange("p n t -> p (n t)").bitcast(I32))
+        w2w_raw = load_words(w2_words, "w2w_raw", "raw0")
+        load_scale_rows(nc.sync, xs, x_scales)
         two_l = load_list(two, "two_l")
-        load_weight(w2_words, w2_scales)
         offs_l = load_list(offs, "offs_l")
+        w2s_raw = load_scales(w2_scales, "w2s_raw", nc.vector, nc.sync)
         n2_l = load_list(n2, "n2_l")
-        gain = tile([P, PACK], F32, "gain")
-        nc.gpsimd.dma_start(out=gain[:], in_=gn.rearrange("(p t) o -> p (t o)", t=PACK))
+        w1w_raw = load_words(w1_words, "w1w_raw", "raw1")
+        w1s_raw = load_scales(w1_scales, "w1s_raw", nc.vector, nc.sync)
+        gain = keep.tile([P, PACK], F32, name="gain", tag="warm", align_bytes=64)
+        nc.scalar.dma_start(out=gain[:], in_=gn.rearrange("(p t) o -> p (t o)", t=PACK))
         n1_l = load_list(n1, "n1_l")
+        w3w_raw = load_words(w3_words, "w3w_raw", "raw2")
+        w3s_raw = load_scales(w3_scales, "w3s_raw", nc.vector, nc.sync)
         n3_l = load_list(n3, "n3_l")
         n4_l = load_list(n4, "n4_l")
 
-        def pick(lst, name, slots):
-            scales = keep.tile([P, S], U8, name=name + "_scales", tag=slots[0], align_bytes=64)
+        def pick_scales(lst, name, slot):
+            scales = keep.tile([P, S], U8, name=name, tag=slot, align_bytes=64)
             nc.vector.tensor_copy(out=scales[:], in_=xs[:].indirect(lst[:]))
-            words = keep.tile([P, S], U32, name=name + "_words", tag=slots[1], align_bytes=64)
-            nc.vector.tensor_copy(out=words[:], in_=xw[:].bitcast(U32).indirect(lst[:]))
-            return words, scales
+            return scales
 
-        def product(w, t, words, scales):
-            bank = psum.tile([P, words.shape[1]], F32, name="bank")
+        def pick_words(lst, name, slot):
+            words = keep.tile([P, S], U32, name=name, tag=slot, align_bytes=64)
+            nc.vector.tensor_copy(out=words[:], in_=xw[:].bitcast(U32).indirect(lst[:]))
+            return words
+
+        def bank_tile(shape, bank):
+            return psum.tile(shape, F32, name="bank%d" % bank)
+
+        def product(w, t, words, scales, where):
+            bank = bank_tile([P, words.shape[1]], where)
             nc.tensor.matmul_mx(
                 out=bank[:],
                 lhsT=w[0][:, t, :, :].rearrange("p m b -> p (m b)").bitcast(FP4X4),
@@ -100,83 +121,127 @@ def tile_picked_twlpullbkind_none_po_kernel(
             )
             return bank
 
-        w2 = deal("w2")
-        load_weight(w1_words, w1_scales)
-        x_two = pick(two_l, "x_two", ("table1", "table2"))
-        x_idx = pick(offs_l, "x_idx", ("table3", "idx_words"))
-        d_win, d_plain = [], []
+        w2w = deal_words(nc.vector, w2w_raw, "w2w")
+        two_scales = pick_scales(two_l, "two_scales", "table1")
+        x_two = (pick_words(two_l, "two_words", "table2"), two_scales)
+        w2 = (w2w, deal_scales(nc.vector, w2s_raw, "w2s"))
+        idx_scales = pick_scales(offs_l, "idx_scales", "table3")
+        x_idx = (pick_words(offs_l, "idx_words", "w2s_raw"), idx_scales)
+        w1w = deal_words(nc.vector, w1w_raw, "w1w")
+        d_win = [tile([P, 2 * S], F32, "d_win%d" % t) for t in range(PACK)]
+        nc.vector.memset(d_win[0][:, S:], 0.0)
+        d_last = tile([P, S], F32, "d_last")
+        d_plain = [win[:, S:] for win in d_win[1:]] + [d_last[:]]
         for t in range(PACK):
-            bank = product(w2, t, *x_two)
-            win = tile([P, S], F32, "d_win%d" % t)
-            nc.scalar.copy(out=win[:], in_=bank[:])
-            plain = tile([P, S], F32, "d_plain%d" % t)
-            nc.scalar.copy(out=plain[:], in_=bank[:])
-            d_win.append(win)
-            d_plain.append(plain)
-        w1 = deal("w1")
-        load_weight(w3_words, w3_scales)
+            bank = product(w2, t, *x_two, t)
+            nc.scalar.copy(out=d_win[t][:, :S], in_=bank[:])
+            nc.scalar.copy(out=d_plain[t], in_=bank[:])
         tab_rows = tab.rearrange("(p t) c -> p t c", t=PACK)
         tab_win = []
         for t in range(PACK):
             win = keep.tile([P, J], F32, name="tab_win%d" % t, tag="table%d" % t, align_bytes=64)
             nc.sync.dma_start(out=win[:], in_=tab_rows[:, t, :])
             tab_win.append(win)
-        gate, y_win = [], []
+        w1 = (w1w, deal_scales(nc.vector, w1s_raw, "w1s"))
+        y_win = []
         for t in range(PACK):
-            diff = tile([P, S], F32, "diff%d" % t)
-            for lo in (0, HALF):
-                cols = slice(lo, lo + HALF)
-                nc.vector.tensor_tensor(diff[:, cols], d_win[t][:].indirect(entries(n2_l, lo, lo + HALF)), d_plain[t][:, cols], ALU.subtract)
-            gate.append(diff)
+            bank = product(w1, t, *x_idx, PACK + t)
+            y_win.append(tile([P, S], F32, "y_win%d" % t))
+            nc.scalar.activation(y_win[t][:], bank[:], ACT.Copy, scale=gain[:, t : t + 1])
+        diff = tile([P, PACK, S], F32, "diff")
         for t in range(PACK):
-            bank = product(w1, t, *x_idx)
-            g = tile([P, S], F32, "gate%d" % t)
-            nc.scalar.activation(g[:], gate[t][:], ACT.Sigmoid)
-            gate[t] = g
-            win = tile([P, S], F32, "y_win%d" % t)
-            nc.scalar.activation(win[:], bank[:], ACT.Copy, scale=gain[:, t : t + 1])
-            y_win.append(win)
-        w3 = deal("w3")
-
+            nc.vector.tensor_tensor(diff[:, t, :], d_win[t][:].indirect(n2_l[:]), d_plain[t], ALU.subtract)
+        first = PIECES[0][1]
+        gate_first = tile([P, 2, PACK, first], F32, "gate_first")
+        gate_rest = tile([P, 2, PACK, S - first], F32, "gate_rest")
+        for t in range(PACK):
+            for side, sign in enumerate((1.0, -1.0)):
+                nc.scalar.activation(gate_first[:, side, t, :], diff[:, t, :first], ACT.Sigmoid, scale=sign)
+        for side, sign in enumerate((1.0, -1.0)):
+            nc.scalar.activation(gate_rest[:, side, :, :], diff[:, :, first:], ACT.Sigmoid, scale=sign)
+        w3 = (deal_words(nc.vector, w3w_raw, "w3w", "d_win0"), deal_scales(nc.vector, w3s_raw, "w3s", "d_win1"))
         h_win = [tile([P, S], F32, "h_win%d" % t) for t in range(PACK)]
-        for lo in (0, HALF):
-            cols = slice(lo, lo + HALF)
-            pulled = tile([P, PACK, HALF], F32, "pulled%d" % lo)
-            kept = tile([P, PACK, HALF], F32, "kept%d" % lo)
+        def mix(piece, t, sums, both):
+            lo, hi = PIECES[piece]
+            pulled, dropped = both[:, 0, :], both[:, 1, :]
+            gate = gate_first[:, :, t, :] if piece == 0 else gate_rest[:, :, t, lo - first : hi - first]
+            nc.vector.tensor_tensor(pulled, y_win[t][:].indirect(entries(n1_l, lo, hi)), gate[:, 0, :], ALU.mult)
+            nc.vector.tensor_tensor(dropped, y_win[t][:, lo:hi], gate[:, 1, :], ALU.mult)
+            for c, total in enumerate(sums):
+                block = slice(c * P, (c + 1) * P)
+                terms = (pulled[:, block], dropped[:, block])
+                for i, term in enumerate(terms):
+                    nc.tensor.matmul(total[:, t, :], term, ident[:], is_transpose=True, start=i == 0, stop=i == len(terms) - 1)
+
+        def turn_back(piece, sums, banks):
+            z = tile([P, len(sums) * P, 2], F32, "z%d" % piece)
+            turned = []
+            for c, total in enumerate(sums):
+                turned.append(tile([P, 2, P, 2], BF16, "turned%d_%d" % (piece, c)))
+                nc.scalar.copy(out=turned[c][:], in_=total[:].rearrange("j (u e) m -> j u m e", e=2))
+            for c, bank in enumerate(banks):
+                pairs = turned[c][:].rearrange("j u m e -> j (u m e)").bitcast(F32)
+                back = bank_tile([P, 2, P], bank)
+                for u in range(2):
+                    nc.tensor.transpose(back[:, u, :], pairs[:, u * P : (u + 1) * P], ident[:])
+                nc.scalar.copy(out=z[:, c * P : (c + 1) * P, :], in_=back[:].rearrange("p u j -> p j u"))
+            return z
+
+        def project(piece, z):
+            lo, hi = PIECES[piece]
+            z_words = tile([P, hi - lo], U32, "z_words%d" % piece)
+            z_scales = tile([P, hi - lo], U8, "z_scales%d" % piece)
+            nc.vector.quantize_mx(out=z_words[:].bitcast(FP8X4), scales=z_scales[:], in_=z[:].rearrange("p c u -> p (c u)").bitcast(BF16))
             for t in range(PACK):
-                nc.vector.tensor_tensor(pulled[:, t, :], y_win[t][:].indirect(entries(n1_l, lo, lo + HALF)), gate[t][:, cols], ALU.mult)
-                nc.vector.scalar_tensor_tensor(kept[:, t, :], gate[t][:, cols], 1.0, y_win[t][:, cols], ALU.subtract, ALU.mult)
-            z = tile([P, HALF, PACK], BF16, "z%d" % lo)
-            nc.vector.tensor_tensor(
-                z[:].rearrange("p (c i) t -> p c t i", i=4),
-                pulled[:].rearrange("p t (c i) -> p c t i", i=4),
-                kept[:].rearrange("p t (c i) -> p c t i", i=4),
-                ALU.subtract,
-            )
-            z_words = tile([P, HALF], U32, "z_words%d" % lo)
-            z_scales = tile([P, HALF], U8, "z_scales%d" % lo)
-            nc.vector.quantize_mx(out=z_words[:].bitcast(FP8X4), scales=z_scales[:], in_=z[:].rearrange("p c t -> p (c t)"))
-            for t in range(PACK):
-                bank = product(w3, t, z_words, z_scales)
-                nc.scalar.copy(out=h_win[t][:, cols], in_=bank[:])
+                bank = product(w3, t, z_words, z_scales, PACK + t)
+                nc.scalar.copy(out=h_win[t][:, lo:hi], in_=bank[:])
+
+        def terms_tile(piece, t):
+            lo, hi = PIECES[piece]
+            return tile([P, 2, hi - lo], F32, "terms%d_%d" % (piece, t))
+
+        sums0 = [bank_tile([P, PACK, P], 0), bank_tile([P, PACK, P], 1)]
+        for t in range(PACK):
+            mix(0, t, sums0, terms_tile(0, t))
+        z0 = turn_back(0, sums0, (2, 3))
+        sums1 = [bank_tile([P, PACK, P], 1)]
+        for t in range(PACK):
+            mix(1, t, sums1, terms_tile(1, t))
+        z1 = turn_back(1, sums1, (0,))
+        project(0, z0)
+        sums2 = [bank_tile([P, PACK, P], 3)]
+        for t in (0, 1):
+            mix(2, t, sums2, terms_tile(2, t))
+        late_terms = tile([P, 2, 2, P], F32, "late_terms", "z0")
+        for t in (2, 3):
+            mix(2, t, sums2, late_terms[:, t - 2, :, :])
+        z2 = turn_back(2, sums2, (2,))
+        project(1, z1)
+        project(2, z2)
 
         out_rows = out_0.rearrange("(p t) c -> p t c", t=PACK)
         out_words = tile([P, S], U32, "out_words")
         out_scales = tile([P, S], U8, "out_scales")
         words_dram = out_1[0].rearrange("p n t -> p (n t)").bitcast(I32)
-        for lo, hi in PIECES:
+
+        def add_table(piece, slot):
+            lo, hi = PIECES[piece]
+            summed = tile([P, PACK, hi - lo], F32, "summed%d" % piece, slot)
+            for t in range(PACK):
+                nc.vector.tensor_tensor(summed[:, t, :], tab_win[t][:].indirect(entries(n3_l, lo, hi)), h_win[t][:, lo:hi], ALU.add)
+            return summed
+
+        def finish(piece, summed, slot):
+            lo, hi = PIECES[piece]
             cols = slice(lo, hi)
             width = hi - lo
-            summed = tile([P, PACK, width], F32, "summed%d" % lo)
-            other = tile([P, PACK, width], F32, "other%d" % lo)
-            for t in range(PACK):
-                nc.vector.tensor_tensor(summed[:, t, :], tab_win[t][:].indirect(entries(n3_l, lo, hi)), h_win[t][:, cols], ALU.add)
+            other = tile([P, PACK, width], F32, "other%d" % piece)
             for t in range(PACK):
                 nc.vector.tensor_copy(out=other[:, t, :], in_=h_win[t][:].indirect(entries(n4_l, lo, hi)))
-            result = tile([P, PACK, width], F32, "result%d" % lo)
+            result = tile([P, PACK, width], F32, "result%d" % piece, slot)
             nc.vector.tensor_tensor(result[:], summed[:], other[:], ALU.max)
             nc.sync.dma_start(out=out_rows[:, :, cols], in_=result[:])
-            rounded = tile([P, width, PACK], BF16, "rounded%d" % lo)
+            rounded = tile([P, width, PACK], BF16, "rounded%d" % piece)
             dst = rounded[:].rearrange("p (c i) t -> p c t i", i=4)
             src = result[:].rearrange("p t (c i) -> p c t i", i=4)
             if hi < S:
@@ -185,6 +250,12 @@ def tile_picked_twlpullbkind_none_po_kernel(
                 nc.vector.tensor_copy(out=dst, in_=src)
             nc.vector.quantize_mx(out=out_words[:, cols].bitcast(FP8X4), scales=out_scales[:, cols], in_=rounded[:].rearrange("p c t -> p (c t)"))
             nc.sync.dma_start(out=words_dram[:, cols], in_=out_words[:, cols].bitcast(I32))
+
+        summed0 = add_table(0, "summed0")
+        summed1 = add_table(1, "z2")
+        finish(0, summed0, "result0")
+        finish(1, summed1, "result1")
+        finish(2, add_table(2, "rounded0"), "rounded1")
         for q in range(4):
             queue = nc.scalar if q % 2 == 0 else nc.sync
             queue.dma_start(out=out_2[0, 4 * q : 4 * q + 4, :].bitcast(I32), in_=out_scales[32 * q : 32 * q + 4, :].bitcast(I32))

@@ -1,7 +1,6 @@
 from contextlib import ExitStack
 
 import concourse.mybir as mybir
-from concourse.masks import make_identity
 
 K, T, S, N, H, J = 512, 2048, 512, 512, 512, 512
 FLOPS = 2 * S * (K * H + K * H + H * N)
@@ -19,7 +18,8 @@ ACT = mybir.ActivationFunctionType
 
 P = 128
 PACK = 4
-PIECES = ((0, 256), (256, 384), (384, 512))
+HALF = S // 2
+BODY = S - P
 
 
 def tile_picked_twlpullbkind_none_po_kernel(
@@ -57,9 +57,6 @@ def tile_picked_twlpullbkind_none_po_kernel(
         warm = tile([P, 2], F32, "warm")
         nc.vector.memset(warm[:, 0:1], 0.0)
         nc.scalar.activation(warm[:, 1:2], warm[:, 0:1], ACT.Sigmoid)
-
-        ident = tile([P, P], F32, "ident")
-        make_identity(nc, ident[:])
 
         xw = keep.tile([P, T], I32, name="xw", tag="table0", align_bytes=64)
 
@@ -143,119 +140,96 @@ def tile_picked_twlpullbkind_none_po_kernel(
             nc.sync.dma_start(out=win[:], in_=tab_rows[:, t, :])
             tab_win.append(win)
         w1 = (w1w, deal_scales(nc.vector, w1s_raw, "w1s"))
-        y_win = []
+        y_win = [tile([P, 2 * S], F32, "y_win%d" % t) for t in range(PACK)]
+        h_win = [tile([P, 2 * S], F32, "h_win%d" % t) for t in range(PACK)]
+        gate = [win[:, S:] for win in h_win]
+        for t in range(PACK):
+            nc.vector.tensor_tensor(y_win[t][:, S:], d_win[t][:].indirect(n2_l[:]), d_plain[t], ALU.subtract)
         for t in range(PACK):
             bank = product(w1, t, *x_idx, PACK + t)
-            y_win.append(tile([P, S], F32, "y_win%d" % t))
-            nc.scalar.activation(y_win[t][:], bank[:], ACT.Copy, scale=gain[:, t : t + 1])
-        diff = tile([P, PACK, S], F32, "diff")
-        for t in range(PACK):
-            nc.vector.tensor_tensor(diff[:, t, :], d_win[t][:].indirect(n2_l[:]), d_plain[t], ALU.subtract)
-        first = PIECES[0][1]
-        gate_first = tile([P, 2, PACK, first], F32, "gate_first")
-        gate_rest = tile([P, 2, PACK, S - first], F32, "gate_rest")
-        for t in range(PACK):
-            for side, sign in enumerate((1.0, -1.0)):
-                nc.scalar.activation(gate_first[:, side, t, :], diff[:, t, :first], ACT.Sigmoid, scale=sign)
-        for side, sign in enumerate((1.0, -1.0)):
-            nc.scalar.activation(gate_rest[:, side, :, :], diff[:, :, first:], ACT.Sigmoid, scale=sign)
+            nc.scalar.activation(gate[t], y_win[t][:, S:], ACT.Sigmoid)
+            nc.scalar.activation(y_win[t][:, :S], bank[:], ACT.Copy, scale=gain[:, t : t + 1])
         w3 = (deal_words(nc.vector, w3w_raw, "w3w", "d_win0"), deal_scales(nc.vector, w3s_raw, "w3s", "d_win1"))
-        h_win = [tile([P, S], F32, "h_win%d" % t) for t in range(PACK)]
-        def mix(piece, t, sums, both):
-            lo, hi = PIECES[piece]
-            pulled, dropped = both[:, 0, :], both[:, 1, :]
-            gate = gate_first[:, :, t, :] if piece == 0 else gate_rest[:, :, t, lo - first : hi - first]
-            nc.vector.tensor_tensor(pulled, y_win[t][:].indirect(entries(n1_l, lo, hi)), gate[:, 0, :], ALU.mult)
-            nc.vector.tensor_tensor(dropped, y_win[t][:, lo:hi], gate[:, 1, :], ALU.mult)
-            for c, total in enumerate(sums):
-                block = slice(c * P, (c + 1) * P)
-                terms = (pulled[:, block], dropped[:, block])
-                for i, term in enumerate(terms):
-                    nc.tensor.matmul(total[:, t, :], term, ident[:], is_transpose=True, start=i == 0, stop=i == len(terms) - 1)
 
-        def turn_back(piece, sums, banks):
-            z = tile([P, len(sums) * P, 2], F32, "z%d" % piece)
-            turned = []
-            for c, total in enumerate(sums):
-                turned.append(tile([P, 2, P, 2], BF16, "turned%d_%d" % (piece, c)))
-                nc.scalar.copy(out=turned[c][:], in_=total[:].rearrange("j (u e) m -> j u m e", e=2))
-            for c, bank in enumerate(banks):
-                pairs = turned[c][:].rearrange("j u m e -> j (u m e)").bitcast(F32)
-                back = bank_tile([P, 2, P], bank)
-                for u in range(2):
-                    nc.tensor.transpose(back[:, u, :], pairs[:, u * P : (u + 1) * P], ident[:])
-                nc.scalar.copy(out=z[:, c * P : (c + 1) * P, :], in_=back[:].rearrange("p u j -> p j u"))
+        pulled = tile([P, PACK, S], F32, "pulled")
+        kept = tile([P, PACK, S], F32, "kept")
+
+        def pull(t, lo, hi):
+            nc.vector.tensor_tensor(pulled[:, t, lo:hi], y_win[t][:].indirect(entries(n1_l, lo, hi)), gate[t][:, lo:hi], ALU.mult)
+
+        def keep_rest(t, lo, hi):
+            nc.vector.scalar_tensor_tensor(kept[:, t, lo:hi], gate[t][:, lo:hi], 1.0, y_win[t][:, lo:hi], ALU.subtract, ALU.mult)
+
+        def mix(lo):
+            z = tile([P, HALF, PACK], BF16, "z%d" % lo)
+            nc.vector.tensor_tensor(
+                z[:].rearrange("p (c i) t -> p c t i", i=4),
+                pulled[:, :, lo : lo + HALF].rearrange("p t (c i) -> p c t i", i=4),
+                kept[:, :, lo : lo + HALF].rearrange("p t (c i) -> p c t i", i=4),
+                ALU.subtract,
+            )
             return z
 
-        def project(piece, z):
-            lo, hi = PIECES[piece]
-            z_words = tile([P, hi - lo], U32, "z_words%d" % piece)
-            z_scales = tile([P, hi - lo], U8, "z_scales%d" % piece)
-            nc.vector.quantize_mx(out=z_words[:].bitcast(FP8X4), scales=z_scales[:], in_=z[:].rearrange("p c u -> p (c u)").bitcast(BF16))
+        def project(lo, z, first_bank):
+            z_words = tile([P, HALF], U32, "z_words%d" % lo)
+            z_scales = tile([P, HALF], U8, "z_scales%d" % lo)
+            nc.vector.quantize_mx(out=z_words[:].bitcast(FP8X4), scales=z_scales[:], in_=z[:].rearrange("p c t -> p (c t)"))
             for t in range(PACK):
-                bank = product(w3, t, z_words, z_scales, PACK + t)
-                nc.scalar.copy(out=h_win[t][:, lo:hi], in_=bank[:])
+                bank = product(w3, t, z_words, z_scales, first_bank + t)
+                nc.scalar.copy(out=h_win[t][:, lo : lo + HALF], in_=bank[:])
 
-        def terms_tile(piece, t):
-            lo, hi = PIECES[piece]
-            return tile([P, 2, hi - lo], F32, "terms%d_%d" % (piece, t))
+        summed = tile([P, PACK, BODY], F32, "summed")
 
-        sums0 = [bank_tile([P, PACK, P], 0), bank_tile([P, PACK, P], 1)]
+        def add_table(t, lo, hi, dst):
+            nc.vector.tensor_tensor(dst, tab_win[t][:].indirect(entries(n3_l, lo, hi)), h_win[t][:, lo:hi], ALU.add)
+
+        last = PACK - 1
+        for t in range(last):
+            pull(t, 0, S)
+            keep_rest(t, 0, S)
+        pull(last, 0, HALF)
+        keep_rest(last, 0, HALF)
+        pull(last, HALF, S)
+        z_first = mix(0)
+        keep_rest(last, HALF, S)
+        project(0, z_first, 0)
+        z_second = mix(HALF)
+        add_table(0, 0, HALF, summed[:, 0, :HALF])
+        project(HALF, z_second, PACK)
+        for t in range(1, PACK):
+            add_table(t, 0, HALF, summed[:, t, :HALF])
         for t in range(PACK):
-            mix(0, t, sums0, terms_tile(0, t))
-        z0 = turn_back(0, sums0, (2, 3))
-        sums1 = [bank_tile([P, PACK, P], 1)]
+            add_table(t, HALF, BODY, summed[:, t, HALF:])
+        other = tile([P, PACK, S], F32, "other")
         for t in range(PACK):
-            mix(1, t, sums1, terms_tile(1, t))
-        z1 = turn_back(1, sums1, (0,))
-        project(0, z0)
-        sums2 = [bank_tile([P, PACK, P], 3)]
-        for t in (0, 1):
-            mix(2, t, sums2, terms_tile(2, t))
-        late_terms = tile([P, 2, 2, P], F32, "late_terms", "z0")
-        for t in (2, 3):
-            mix(2, t, sums2, late_terms[:, t - 2, :, :])
-        z2 = turn_back(2, sums2, (2,))
-        project(1, z1)
-        project(2, z2)
+            nc.vector.tensor_copy(out=other[:, t, :], in_=h_win[t][:].indirect(n4_l[:]))
 
         out_rows = out_0.rearrange("(p t) c -> p t c", t=PACK)
         out_words = tile([P, S], U32, "out_words")
         out_scales = tile([P, S], U8, "out_scales")
         words_dram = out_1[0].rearrange("p n t -> p (n t)").bitcast(I32)
 
-        def add_table(piece, slot):
-            lo, hi = PIECES[piece]
-            summed = tile([P, PACK, hi - lo], F32, "summed%d" % piece, slot)
-            for t in range(PACK):
-                nc.vector.tensor_tensor(summed[:, t, :], tab_win[t][:].indirect(entries(n3_l, lo, hi)), h_win[t][:, lo:hi], ALU.add)
-            return summed
+        def larger(lo, hi, sums):
+            result = tile([P, PACK, hi - lo], F32, "result%d" % lo)
+            nc.vector.tensor_tensor(result[:], sums, other[:, :, lo:hi], ALU.max)
+            nc.sync.dma_start(out=out_rows[:, :, lo:hi], in_=result[:])
+            return result
 
-        def finish(piece, summed, slot):
-            lo, hi = PIECES[piece]
-            cols = slice(lo, hi)
-            width = hi - lo
-            other = tile([P, PACK, width], F32, "other%d" % piece)
-            for t in range(PACK):
-                nc.vector.tensor_copy(out=other[:, t, :], in_=h_win[t][:].indirect(entries(n4_l, lo, hi)))
-            result = tile([P, PACK, width], F32, "result%d" % piece, slot)
-            nc.vector.tensor_tensor(result[:], summed[:], other[:], ALU.max)
-            nc.sync.dma_start(out=out_rows[:, :, cols], in_=result[:])
-            rounded = tile([P, width, PACK], BF16, "rounded%d" % piece)
-            dst = rounded[:].rearrange("p (c i) t -> p c t i", i=4)
-            src = result[:].rearrange("p t (c i) -> p c t i", i=4)
-            if hi < S:
-                nc.scalar.copy(out=dst, in_=src)
-            else:
-                nc.vector.tensor_copy(out=dst, in_=src)
-            nc.vector.quantize_mx(out=out_words[:, cols].bitcast(FP8X4), scales=out_scales[:, cols], in_=rounded[:].rearrange("p c t -> p (c t)"))
-            nc.sync.dma_start(out=words_dram[:, cols], in_=out_words[:, cols].bitcast(I32))
+        def planes(values, lo, hi, copy):
+            rounded = tile([P, hi - lo, PACK], BF16, "rounded%d" % lo)
+            copy(out=rounded[:].rearrange("p (c i) t -> p c t i", i=4), in_=values.rearrange("p t (c i) -> p c t i", i=4))
+            nc.vector.quantize_mx(out=out_words[:, lo:hi].bitcast(FP8X4), scales=out_scales[:, lo:hi], in_=rounded[:].rearrange("p c t -> p (c t)"))
 
-        summed0 = add_table(0, "summed0")
-        summed1 = add_table(1, "z2")
-        finish(0, summed0, "result0")
-        finish(1, summed1, "result1")
-        finish(2, add_table(2, "rounded0"), "rounded1")
+        body = larger(0, BODY, summed[:])
+        tail_sums = h_win[last][:, S:].rearrange("p (t c) -> p t c", t=PACK)
+        for t in range(PACK):
+            add_table(t, BODY, S, tail_sums[:, t, :])
+        planes(body[:, :, :HALF], 0, HALF, nc.scalar.copy)
+        tail = larger(BODY, S, tail_sums)
+        planes(body[:, :, HALF:], HALF, BODY, nc.scalar.copy)
+        nc.sync.dma_start(out=words_dram[:, :BODY], in_=out_words[:, :BODY].bitcast(I32))
+        planes(tail[:], BODY, S, nc.vector.tensor_copy)
+        nc.sync.dma_start(out=words_dram[:, BODY:], in_=out_words[:, BODY:].bitcast(I32))
         for q in range(4):
             queue = nc.scalar if q % 2 == 0 else nc.sync
             queue.dma_start(out=out_2[0, 4 * q : 4 * q + 4, :].bitcast(I32), in_=out_scales[32 * q : 32 * q + 4, :].bitcast(I32))

from contextlib import ExitStack

import concourse.mybir as mybir

K, T, S, N, H, J = 512, 2048, 512, 512, 512, 512
FLOPS = 2 * S * (K * H + K * H + H * N)

F32 = mybir.dt.float32
BF16 = mybir.dt.bfloat16
I32 = mybir.dt.int32
U32 = mybir.dt.uint32
U16 = mybir.dt.uint16
U8 = mybir.dt.uint8
FP8X4 = mybir.dt.float8_e4m3fn_x4
FP4X4 = mybir.dt.float4_e2m1fn_x4
ALU = mybir.AluOpType
ACT = mybir.ActivationFunctionType

P = 128
PACK = 4
HALF = S // 2
BODY = S - P


def tile_picked_twlpullbkind_none_po_kernel(
    tc, x_words, x_scales, w1_words, w1_scales, w2_words, w2_scales, gn, w3_words, w3_scales,
    tab, offs, two, n1, n2, n3, n4, out_0, out_1, out_2,
):
    nc = tc.nc
    with ExitStack() as ctx:
        keep = ctx.enter_context(tc.tile_pool(name="keep", bufs=1))
        psum = ctx.enter_context(tc.psum_pool(name="psum", bufs=1))

        def tile(shape, dtype, name, slot=None):
            return keep.tile(shape, dtype, name=name, tag=slot or name, align_bytes=64)

        def load_list(src, name):
            dst = tile([P, S // 16], U16, name)
            nc.sync.dma_start(dst[:], src)
            return dst

        def load_scale_rows(queue, dst, src):
            for q in range(4):
                queue.dma_start(out=dst[32 * q : 32 * q + 4, :].bitcast(I32), in_=src[0, 4 * q : 4 * q + 4, :].bitcast(I32))

        def entries(lst, lo, hi):
            return lst[:, lo // 16 : hi // 16]

        def load_scales(src, name, engine, queue):
            raw = tile([P, H], U8, name)
            engine.memset(raw[:].bitcast(I32), 0)
            load_scale_rows(queue, raw, src)
            return raw

        xs = tile([P, T], U8, "xs")
        nc.vector.memset(xs[:].bitcast(I32), 0)
        warm = tile([P, 2], F32, "warm")
        nc.vector.memset(warm[:, 0:1], 0.0)
        nc.scalar.activation(warm[:, 1:2], warm[:, 0:1], ACT.Sigmoid)

        xw = keep.tile([P, T], I32, name="xw", tag="table0", align_bytes=64)

        def load_words(src, name, slot):
            raw = keep.tile([P, 2 * H], U8, name=name, tag=slot, align_bytes=64)
            nc.sync.dma_start(out=raw[:].bitcast(I32), in_=src[0].bitcast(I32))
            return raw

        def deal_words(engine, raw, name, slot=None):
            words = tile([P, PACK, P, 2], U8, name, slot)
            engine.tensor_copy(out=words[:], in_=raw[:].rearrange("p (m t b) -> p t m b", t=PACK, b=2))
            return words

        def deal_scales(engine, raw, name, slot=None):
            scales = tile([P, PACK, P], U8, name, slot)
            engine.tensor_copy(out=scales[:], in_=raw[:].rearrange("p (m t) -> p t m", t=PACK))
            return scales

        nc.scalar.dma_start(out=xw[:], in_=x_words[0].rearrange("p n t -> p (n t)").bitcast(I32))
        w2w_raw = load_words(w2_words, "w2w_raw", "raw0")
        load_scale_rows(nc.sync, xs, x_scales)
        two_l = load_list(two, "two_l")
        offs_l = load_list(offs, "offs_l")
        w2s_raw = load_scales(w2_scales, "w2s_raw", nc.vector, nc.sync)
        n2_l = load_list(n2, "n2_l")
        w1w_raw = load_words(w1_words, "w1w_raw", "raw1")
        w1s_raw = load_scales(w1_scales, "w1s_raw", nc.vector, nc.sync)
        gain = keep.tile([P, PACK], F32, name="gain", tag="warm", align_bytes=64)
        nc.scalar.dma_start(out=gain[:], in_=gn.rearrange("(p t) o -> p (t o)", t=PACK))
        n1_l = load_list(n1, "n1_l")
        w3w_raw = load_words(w3_words, "w3w_raw", "raw2")
        w3s_raw = load_scales(w3_scales, "w3s_raw", nc.vector, nc.sync)
        n3_l = load_list(n3, "n3_l")
        n4_l = load_list(n4, "n4_l")

        def pick_scales(lst, name, slot):
            scales = keep.tile([P, S], U8, name=name, tag=slot, align_bytes=64)
            nc.vector.tensor_copy(out=scales[:], in_=xs[:].indirect(lst[:]))
            return scales

        def pick_words(lst, name, slot):
            words = keep.tile([P, S], U32, name=name, tag=slot, align_bytes=64)
            nc.vector.tensor_copy(out=words[:], in_=xw[:].bitcast(U32).indirect(lst[:]))
            return words

        def bank_tile(shape, bank):
            return psum.tile(shape, F32, name="bank%d" % bank)

        def product(w, t, words, scales, where):
            bank = bank_tile([P, words.shape[1]], where)
            nc.tensor.matmul_mx(
                out=bank[:],
                lhsT=w[0][:, t, :, :].rearrange("p m b -> p (m b)").bitcast(FP4X4),
                lhsT_scale=w[1][:, t, :],
                rhs=words[:].bitcast(FP8X4),
                rhs_scale=scales[:],
                start=True,
                stop=True,
            )
            return bank

        w2w = deal_words(nc.vector, w2w_raw, "w2w")
        two_scales = pick_scales(two_l, "two_scales", "table1")
        x_two = (pick_words(two_l, "two_words", "table2"), two_scales)
        w2 = (w2w, deal_scales(nc.vector, w2s_raw, "w2s"))
        idx_scales = pick_scales(offs_l, "idx_scales", "table3")
        x_idx = (pick_words(offs_l, "idx_words", "w2s_raw"), idx_scales)
        w1w = deal_words(nc.vector, w1w_raw, "w1w")
        d_win = [tile([P, 2 * S], F32, "d_win%d" % t) for t in range(PACK)]
        nc.vector.memset(d_win[0][:, S:], 0.0)
        d_last = tile([P, S], F32, "d_last")
        d_plain = [win[:, S:] for win in d_win[1:]] + [d_last[:]]
        for t in range(PACK):
            bank = product(w2, t, *x_two, t)
            nc.scalar.copy(out=d_win[t][:, :S], in_=bank[:])
            nc.scalar.copy(out=d_plain[t], in_=bank[:])
        tab_rows = tab.rearrange("(p t) c -> p t c", t=PACK)
        tab_win = []
        for t in range(PACK):
            win = keep.tile([P, J], F32, name="tab_win%d" % t, tag="table%d" % t, align_bytes=64)
            nc.sync.dma_start(out=win[:], in_=tab_rows[:, t, :])
            tab_win.append(win)
        w1 = (w1w, deal_scales(nc.vector, w1s_raw, "w1s"))
        y_win = [tile([P, 2 * S], F32, "y_win%d" % t) for t in range(PACK)]
        h_win = [tile([P, 2 * S], F32, "h_win%d" % t) for t in range(PACK)]
        gate = [win[:, S:] for win in h_win]
        for t in range(PACK):
            nc.vector.tensor_tensor(y_win[t][:, S:], d_win[t][:].indirect(n2_l[:]), d_plain[t], ALU.subtract)
        for t in range(PACK):
            bank = product(w1, t, *x_idx, PACK + t)
            nc.scalar.activation(gate[t], y_win[t][:, S:], ACT.Sigmoid)
            nc.scalar.activation(y_win[t][:, :S], bank[:], ACT.Copy, scale=gain[:, t : t + 1])
        w3 = (deal_words(nc.vector, w3w_raw, "w3w", "d_win0"), deal_scales(nc.vector, w3s_raw, "w3s", "d_win1"))

        pulled = tile([P, PACK, S], F32, "pulled")
        kept = tile([P, PACK, S], F32, "kept")

        def pull(t, lo, hi):
            nc.vector.tensor_tensor(pulled[:, t, lo:hi], y_win[t][:].indirect(entries(n1_l, lo, hi)), gate[t][:, lo:hi], ALU.mult)

        def keep_rest(t, lo, hi):
            nc.vector.scalar_tensor_tensor(kept[:, t, lo:hi], gate[t][:, lo:hi], 1.0, y_win[t][:, lo:hi], ALU.subtract, ALU.mult)

        def mix(lo):
            z = tile([P, HALF, PACK], BF16, "z%d" % lo)
            nc.vector.tensor_tensor(
                z[:].rearrange("p (c i) t -> p c t i", i=4),
                pulled[:, :, lo : lo + HALF].rearrange("p t (c i) -> p c t i", i=4),
                kept[:, :, lo : lo + HALF].rearrange("p t (c i) -> p c t i", i=4),
                ALU.subtract,
            )
            return z

        def project(lo, z, first_bank):
            z_words = tile([P, HALF], U32, "z_words%d" % lo)
            z_scales = tile([P, HALF], U8, "z_scales%d" % lo)
            nc.vector.quantize_mx(out=z_words[:].bitcast(FP8X4), scales=z_scales[:], in_=z[:].rearrange("p c t -> p (c t)"))
            for t in range(PACK):
                bank = product(w3, t, z_words, z_scales, first_bank + t)
                nc.scalar.copy(out=h_win[t][:, lo : lo + HALF], in_=bank[:])

        summed = tile([P, PACK, BODY], F32, "summed")

        def add_table(t, lo, hi, dst):
            nc.vector.tensor_tensor(dst, tab_win[t][:].indirect(entries(n3_l, lo, hi)), h_win[t][:, lo:hi], ALU.add)

        last = PACK - 1
        for t in range(last):
            pull(t, 0, S)
            keep_rest(t, 0, S)
        pull(last, 0, HALF)
        keep_rest(last, 0, HALF)
        pull(last, HALF, S)
        z_first = mix(0)
        keep_rest(last, HALF, S)
        project(0, z_first, 0)
        z_second = mix(HALF)
        add_table(0, 0, HALF, summed[:, 0, :HALF])
        project(HALF, z_second, PACK)
        for t in range(1, PACK):
            add_table(t, 0, HALF, summed[:, t, :HALF])
        for t in range(PACK):
            add_table(t, HALF, BODY, summed[:, t, HALF:])
        other = tile([P, PACK, S], F32, "other")
        for t in range(PACK):
            nc.vector.tensor_copy(out=other[:, t, :], in_=h_win[t][:].indirect(n4_l[:]))

        out_rows = out_0.rearrange("(p t) c -> p t c", t=PACK)
        out_words = tile([P, S], U32, "out_words")
        out_scales = tile([P, S], U8, "out_scales")
        words_dram = out_1[0].rearrange("p n t -> p (n t)").bitcast(I32)

        def larger(lo, hi, sums):
            result = tile([P, PACK, hi - lo], F32, "result%d" % lo)
            nc.vector.tensor_tensor(result[:], sums, other[:, :, lo:hi], ALU.max)
            nc.sync.dma_start(out=out_rows[:, :, lo:hi], in_=result[:])
            return result

        def planes(values, lo, hi, copy):
            rounded = tile([P, hi - lo, PACK], BF16, "rounded%d" % lo)
            copy(out=rounded[:].rearrange("p (c i) t -> p c t i", i=4), in_=values.rearrange("p t (c i) -> p c t i", i=4))
            nc.vector.quantize_mx(out=out_words[:, lo:hi].bitcast(FP8X4), scales=out_scales[:, lo:hi], in_=rounded[:].rearrange("p c t -> p (c t)"))

        body = larger(0, BODY, summed[:])
        tail_sums = h_win[last][:, S:].rearrange("p (t c) -> p t c", t=PACK)
        for t in range(PACK):
            add_table(t, BODY, S, tail_sums[:, t, :])
        planes(body[:, :, :HALF], 0, HALF, nc.scalar.copy)
        tail = larger(BODY, S, tail_sums)
        planes(body[:, :, HALF:], HALF, BODY, nc.scalar.copy)
        nc.sync.dma_start(out=words_dram[:, :BODY], in_=out_words[:, :BODY].bitcast(I32))
        planes(tail[:], BODY, S, nc.vector.tensor_copy)
        nc.sync.dma_start(out=words_dram[:, BODY:], in_=out_words[:, BODY:].bitcast(I32))
        for q in range(4):
            queue = nc.scalar if q % 2 == 0 else nc.sync
            queue.dma_start(out=out_2[0, 4 * q : 4 * q + 4, :].bitcast(I32), in_=out_scales[32 * q : 32 * q + 4, :].bitcast(I32))
